import numpy as np
import ml_dtypes


def mxq(x, axis, fmt="e4m3"):
    dtype, down = {"e4m3": (ml_dtypes.float8_e4m3fn, 7), "e5m2": (ml_dtypes.float8_e5m2, 14)}[fmt]
    v = np.moveaxis(np.asarray(x, np.float32).astype(ml_dtypes.bfloat16).astype(np.float64), axis, -1)
    blocks = v.reshape(v.shape[:-1] + (-1, 32))
    amax = np.abs(blocks).max(-1, keepdims=True)
    byte = np.maximum(np.where(amax > 0, np.frexp(amax)[1] - 1 + 127, 0) - down, 1)
    scale = np.exp2(byte - 127.0)
    codes = (blocks / scale).astype(np.float32).astype(dtype).astype(np.float64)
    return np.moveaxis((codes * scale).reshape(v.shape), -1, axis)


WIDE = False


def mx_kscale(k):
    if not WIDE:
        return np.ones(k)
    levels = np.array([10, -10, 5, -5, 0])
    if k % 512:
        return np.exp2(np.random.permutation(np.resize(levels, k // 32))).repeat(32)
    a = np.empty((k // 512, 16))
    for p in range(k // 512):
        a[p, :8] = np.random.permutation(np.resize(levels, 8))
        for g in range(8):
            far = levels[np.abs(levels - a[p, g]) >= 10]
            a[p, g + 8] = far[np.random.randint(len(far))]
    return np.exp2(a.ravel()).repeat(32)


def f64(x):
    return np.asarray(x).astype(np.float64)


def striped(idx):
    return np.tile(np.asarray(idx).reshape(-1, 16).T, (8, 1)).astype(np.uint16)


def unstriped(offs):
    return offs[:16].T.reshape(-1).astype(np.int64)


def striped8(idx):
    return np.asarray(idx).reshape(8, -1, 16).transpose(0, 2, 1).reshape(128, -1).astype(np.uint16)


def unstriped8(offs):
    return offs.reshape(8, 16, -1).transpose(0, 2, 1).reshape(8, -1).astype(np.int64)


def pick8(x, idx, run):
    r = np.arange(len(x))
    return x[r[:, None], idx[r % (8 * run) // run]]


E2M1 = np.array([0.0, 0.5, 1.0, 1.5, 2.0, 3.0, 4.0, 6.0, -0.0, -0.5, -1.0, -1.5, -2.0, -3.0, -4.0, -6.0])


def pack_weight(w, fmt):
    k, n = w.shape
    w = f64(np.asarray(w, np.float32).astype(ml_dtypes.bfloat16)).reshape(k // 32, 32, n)
    amax = np.abs(w).max(1)
    if fmt == "e4m3":
        byte = np.frexp(amax)[1] - 1 + 127 - 7
    else:
        mant, ex = np.frexp(amax / 6.0)
        byte = np.where(mant > 0.5, ex, ex - 1) + 127
    byte = np.clip(np.where(amax > 0, byte, 1), 1, 254)
    scaled = (w * np.exp2(127.0 - byte)[:, None, :]).reshape(k, n).astype(np.float32)
    by_word = np.ascontiguousarray(scaled.reshape(k // 512, 128, 4, n).transpose(0, 1, 3, 2))
    if fmt == "e4m3":
        words = by_word.astype(ml_dtypes.float8_e4m3fn).view(np.uint8)
    else:
        c = by_word.astype(ml_dtypes.float4_e2m1fn).view(np.uint8) & 0xF
        words = (c[..., 0::2] | (c[..., 1::2] << 4)).reshape(k // 512, 128, 2 * n)
    return np.ascontiguousarray(words), np.ascontiguousarray(byte.astype(np.uint8).reshape(k // 512, 16, n))


def unpack_weight(words, scales, fmt):
    g, _, n = scales.shape
    words = np.ascontiguousarray(words).reshape(g, 128, n, -1)
    if fmt == "e4m3":
        vals = words.view(ml_dtypes.float8_e4m3fn).astype(np.float64)
    else:
        nib = np.empty((g, 128, n, 4), np.uint8)
        nib[..., 0::2] = words & 0xF
        nib[..., 1::2] = words >> 4
        vals = E2M1[nib]
    vals = vals * np.repeat(np.exp2(scales.astype(np.float64) - 127.0), 8, axis=1)[..., None]
    return vals.transpose(0, 1, 3, 2).reshape(g * 512, n)


def sgn(shape):
    return np.random.uniform(0.5, 2.0, shape) * np.where(np.random.standard_normal(shape) < 0, -1.0, 1.0)


K, I, C, J, N, E = 512, 256, 512, 256, 256, 512


def setup_inputs():
    n = np.random.standard_normal
    idx = np.stack([np.random.permutation(C)[:I] for _ in range(8)])
    idx2 = np.stack([np.random.permutation(C)[:J] for _ in range(8)])
    idx3 = np.random.permutation(E)[:J]
    fk = mx_kscale(K)
    wp = pack_weight(n((K, N)) * 1 / np.sqrt(K) / fk[:, None], "e2m1")
    return {
        "ca": (np.random.randint(-7, 8, (K, I)).astype(np.float64)).astype(np.float32),
        "sa": (np.random.uniform(0.1, 0.4, (K, 1)) * fk[:, None]).astype(np.float32),
        "w_words": wp[0],
        "w_scales": wp[1],
        "so": (sgn((N, 1))).astype(np.float32),
        "offs": striped8(idx),
        "offs2": striped8(idx2),
        "offs3": striped(idx3),
    }


def reference(ca, sa, w_words, w_scales, so, offs, offs2, offs3):
    idx = unstriped8(offs)
    idx2 = unstriped8(offs2)
    idx3 = unstriped(offs3)
    wu = unpack_weight(w_words, w_scales, "e2m1")
    pg = np.zeros((K, C))
    pg[np.arange(K)[:, None], idx[np.arange(K) % 512 // 64]] = f64(ca) * f64(sa)
    z = pick8(pg, idx2, 64)
    zq = mxq(z, 0, "e4m3")
    p = wu.T @ zq
    y = np.zeros((N, E))
    y[:, idx3] = p * f64(so)
    return y

@@ -1,0 +1,100 @@
+from contextlib import ExitStack
+
+import concourse.mybir as mybir
+
+K, I, C, J, N, E = 512, 256, 512, 256, 256, 512
+FLOPS = 2 * K * N * J
+
+F32 = mybir.dt.float32
+BF16 = mybir.dt.bfloat16
+I32 = mybir.dt.int32
+U32 = mybir.dt.uint32
+U16 = mybir.dt.uint16
+U8 = mybir.dt.uint8
+FP8X4 = mybir.dt.float8_e4m3fn_x4
+FP4X4 = mybir.dt.float4_e2m1fn_x4
+COPY = mybir.ActivationFunctionType.Copy
+
+P = 128
+PACK = 4
+GROUP = 16
+HALVES = 2
+JH = J // HALVES
+N_TILES = N // P
+
+
+def tile_list_ownpagedcodes_kernel(tc, ca, sa, w_words, w_scales, so, offs, offs2, offs3, out):
+    nc = tc.nc
+    with ExitStack() as ctx:
+        keep = ctx.enter_context(tc.tile_pool(name="keep", bufs=1))
+        psum = ctx.enter_context(tc.psum_pool(name="psum", bufs=1))
+
+        put_list = keep.tile([P, I // GROUP], U16, name="put_list")
+        take_list = keep.tile([P, J // GROUP], U16, name="take_list")
+        out_list = keep.tile([P, J // GROUP], U16, name="out_list")
+        ca_first = keep.tile([P, I], F32, name="ca_first", align_bytes=64)
+        ca_rest = keep.tile([P, (PACK - 1) * I], F32, name="ca_rest", align_bytes=64)
+        steps = keep.tile([P, PACK], F32, name="steps")
+        gains = keep.tile([P, N_TILES], F32, name="gains")
+        w_codes = keep.tile([P, 2 * N], U8, name="w_codes", align_bytes=64)
+        w_plane = keep.tile([P, N], U8, name="w_plane", align_bytes=64)
+        pages = [keep.tile([P, C], F32, name=f"page{r}", align_bytes=64) for r in range(PACK)]
+        results = [keep.tile([P, E], F32, name=f"result{t}", align_bytes=64) for t in range(N_TILES)]
+
+        ca_rows = ca.rearrange("(p r) i -> p (r i)", r=PACK)
+        nc.sync.dma_start(ca_first[:], ca_rows[:, 0:I])
+        nc.sync.dma_start(put_list[:], offs)
+        nc.scalar.dma_start(steps[:], sa.rearrange("(p r) o -> p (r o)", r=PACK))
+        nc.sync.dma_start(ca_rest[:], ca_rows[:, I : PACK * I])
+        nc.sync.dma_start(take_list[:], offs2)
+        nc.sync.dma_start(w_codes[:].bitcast(I32), w_words[0].bitcast(I32))
+        nc.sync.dma_start(out_list[:], offs3)
+        with nc.allow_non_contiguous_dma(reason="one gain a partition and output tile"):
+            nc.sync.dma_start(gains[:], so.rearrange("(t p) o -> p (t o)", p=P))
+
+        nc.vector.memset(pages[0][:], 0.0)
+        nc.vector.memset(w_plane[:].bitcast(I32), 0)
+        for r in range(1, PACK):
+            nc.vector.memset(pages[r][:], 0.0)
+        for t in range(N_TILES):
+            nc.vector.memset(results[t][:], 0.0)
+        for q in range(4):
+            nc.sync.dma_start(
+                w_plane[32 * q : 32 * q + 4, :].bitcast(I32), w_scales[0, 4 * q : 4 * q + 4, :].bitcast(I32)
+            )
+
+        for r in range(PACK):
+            rows = ca_first[:] if r == 0 else ca_rest[:, (r - 1) * I : r * I]
+            nc.scalar.activation(pages[r][:].indirect(put_list[:]), rows, COPY, scale=steps[:, r : r + 1])
+
+        sums = {}
+        for h in range(HALVES):
+            cols = slice(h * JH // GROUP, (h + 1) * JH // GROUP)
+            z = keep.tile([P, PACK * JH], BF16, name=f"z{h}", align_bytes=64)
+            z_codes = keep.tile([P, JH], U32, name=f"z_codes{h}", align_bytes=64)
+            z_plane = keep.tile([P, JH], U8, name=f"z_plane{h}", align_bytes=64)
+            for r in range(PACK):
+                nc.scalar.activation(z[:, r : PACK * JH : PACK], pages[r][:].indirect(take_list[:, cols]), COPY)
+            nc.vector.quantize_mx(out=z_codes[:].bitcast(FP8X4), scales=z_plane[:], in_=z[:])
+            for t in range(N_TILES):
+                acc = psum.tile([P, JH], F32, name=f"acc{h}{t}")
+                nc.tensor.matmul_mx(
+                    out=acc[:],
+                    lhsT=w_codes[:, 2 * P * t : 2 * P * (t + 1)].bitcast(FP4X4),
+                    lhsT_scale=w_plane[:, P * t : P * (t + 1)],
+                    rhs=z_codes[:].bitcast(FP8X4),
+                    rhs_scale=z_plane[:],
+                    start=True,
+                    stop=True,
+                )
+                sums[h, t] = keep.tile([P, JH], F32, name=f"sums{h}{t}", align_bytes=64)
+                nc.vector.tensor_copy(sums[h, t][:], acc[:])
+
+        for h in range(HALVES):
+            cols = slice(h * JH // GROUP, (h + 1) * JH // GROUP)
+            for t in range(N_TILES):
+                nc.scalar.activation(
+                    results[t][:].indirect(out_list[:, cols]), sums[h, t][:], COPY, scale=gains[:, t : t + 1]
+                )
+        for t in range(N_TILES):
+            nc.sync.dma_start(out[P * t : P * (t + 1), :], results[t][:])

@@ -52,6 +52,11 @@ def tile_list_ownpagedcodes_kernel(tc, ca, sa, w_words, w_scales, so, offs, offs
         with nc.allow_non_contiguous_dma(reason="one gain a partition and output tile"):
             nc.sync.dma_start(gains[:], so.rearrange("(t p) o -> p (t o)", p=P))
 
+        warm_in = keep.tile([P, 1], F32, name="warm_in")
+        warm_out = keep.tile([P, 1], F32, name="warm_out")
+        nc.vector.memset(warm_in[:], 0.0)
+        nc.scalar.activation(warm_out[:], warm_in[:], COPY)
+
         nc.vector.memset(pages[0][:], 0.0)
         nc.vector.memset(w_plane[:].bitcast(I32), 0)
         for r in range(1, PACK):

@@ -73,11 +73,11 @@ def tile_list_ownpagedcodes_kernel(tc, ca, sa, w_words, w_scales, so, offs, offs
             nc.scalar.activation(pages[r][:].indirect(put_list[:]), rows, COPY, scale=steps[:, r : r + 1])
 
         sums = {}
+        z_codes = keep.tile([P, JH], U32, name="z_codes", align_bytes=64)
+        z_plane = keep.tile([P, JH], U8, name="z_plane", align_bytes=64)
         for h in range(HALVES):
             cols = slice(h * JH // GROUP, (h + 1) * JH // GROUP)
             z = keep.tile([P, PACK * JH], BF16, name=f"z{h}", align_bytes=64)
-            z_codes = keep.tile([P, JH], U32, name=f"z_codes{h}", align_bytes=64)
-            z_plane = keep.tile([P, JH], U8, name=f"z_plane{h}", align_bytes=64)
             for r in range(PACK):
                 nc.scalar.activation(z[:, r : PACK * JH : PACK], pages[r][:].indirect(take_list[:, cols]), COPY)
             nc.vector.quantize_mx(out=z_codes[:].bitcast(FP8X4), scales=z_plane[:], in_=z[:])

@@ -44,7 +44,7 @@ def tile_list_ownpagedcodes_kernel(tc, ca, sa, w_words, w_scales, so, offs, offs
         ca_rows = ca.rearrange("(p r) i -> p (r i)", r=PACK)
         nc.sync.dma_start(ca_first[:], ca_rows[:, 0:I])
         nc.sync.dma_start(put_list[:], offs)
-        nc.scalar.dma_start(steps[:], sa.rearrange("(p r) o -> p (r o)", r=PACK))
+        nc.sync.dma_start(steps[:], sa.rearrange("(p r) o -> p (r o)", r=PACK))
         nc.sync.dma_start(ca_rest[:], ca_rows[:, I : PACK * I])
         nc.sync.dma_start(take_list[:], offs2)
         nc.sync.dma_start(w_codes[:].bitcast(I32), w_words[0].bitcast(I32))

from contextlib import ExitStack

import concourse.mybir as mybir

K, I, C, J, N, E = 512, 256, 512, 256, 256, 512
FLOPS = 2 * K * N * J

F32 = mybir.dt.float32
BF16 = mybir.dt.bfloat16
I32 = mybir.dt.int32
U32 = mybir.dt.uint32
U16 = mybir.dt.uint16
U8 = mybir.dt.uint8
FP8X4 = mybir.dt.float8_e4m3fn_x4
FP4X4 = mybir.dt.float4_e2m1fn_x4
COPY = mybir.ActivationFunctionType.Copy

P = 128
PACK = 4
GROUP = 16
HALVES = 2
JH = J // HALVES
N_TILES = N // P


def tile_list_ownpagedcodes_kernel(tc, ca, sa, w_words, w_scales, so, offs, offs2, offs3, out):
    nc = tc.nc
    with ExitStack() as ctx:
        keep = ctx.enter_context(tc.tile_pool(name="keep", bufs=1))
        psum = ctx.enter_context(tc.psum_pool(name="psum", bufs=1))

        put_list = keep.tile([P, I // GROUP], U16, name="put_list")
        take_list = keep.tile([P, J // GROUP], U16, name="take_list")
        out_list = keep.tile([P, J // GROUP], U16, name="out_list")
        ca_first = keep.tile([P, I], F32, name="ca_first", align_bytes=64)
        ca_rest = keep.tile([P, (PACK - 1) * I], F32, name="ca_rest", align_bytes=64)
        steps = keep.tile([P, PACK], F32, name="steps")
        gains = keep.tile([P, N_TILES], F32, name="gains")
        w_codes = keep.tile([P, 2 * N], U8, name="w_codes", align_bytes=64)
        w_plane = keep.tile([P, N], U8, name="w_plane", align_bytes=64)
        pages = [keep.tile([P, C], F32, name=f"page{r}", align_bytes=64) for r in range(PACK)]
        results = [keep.tile([P, E], F32, name=f"result{t}", align_bytes=64) for t in range(N_TILES)]

        ca_rows = ca.rearrange("(p r) i -> p (r i)", r=PACK)
        nc.sync.dma_start(ca_first[:], ca_rows[:, 0:I])
        nc.sync.dma_start(put_list[:], offs)
        nc.sync.dma_start(steps[:], sa.rearrange("(p r) o -> p (r o)", r=PACK))
        nc.sync.dma_start(ca_rest[:], ca_rows[:, I : PACK * I])
        nc.sync.dma_start(take_list[:], offs2)
        nc.sync.dma_start(w_codes[:].bitcast(I32), w_words[0].bitcast(I32))
        nc.sync.dma_start(out_list[:], offs3)
        with nc.allow_non_contiguous_dma(reason="one gain a partition and output tile"):
            nc.sync.dma_start(gains[:], so.rearrange("(t p) o -> p (t o)", p=P))

        warm_in = keep.tile([P, 1], F32, name="warm_in")
        warm_out = keep.tile([P, 1], F32, name="warm_out")
        nc.vector.memset(warm_in[:], 0.0)
        nc.scalar.activation(warm_out[:], warm_in[:], COPY)

        nc.vector.memset(pages[0][:], 0.0)
        nc.vector.memset(w_plane[:].bitcast(I32), 0)
        for r in range(1, PACK):
            nc.vector.memset(pages[r][:], 0.0)
        for t in range(N_TILES):
            nc.vector.memset(results[t][:], 0.0)
        for q in range(4):
            nc.sync.dma_start(
                w_plane[32 * q : 32 * q + 4, :].bitcast(I32), w_scales[0, 4 * q : 4 * q + 4, :].bitcast(I32)
            )

        for r in range(PACK):
            rows = ca_first[:] if r == 0 else ca_rest[:, (r - 1) * I : r * I]
            nc.scalar.activation(pages[r][:].indirect(put_list[:]), rows, COPY, scale=steps[:, r : r + 1])

        sums = {}
        z_codes = keep.tile([P, JH], U32, name="z_codes", align_bytes=64)
        z_plane = keep.tile([P, JH], U8, name="z_plane", align_bytes=64)
        for h in range(HALVES):
            cols = slice(h * JH // GROUP, (h + 1) * JH // GROUP)
            z = keep.tile([P, PACK * JH], BF16, name=f"z{h}", align_bytes=64)
            for r in range(PACK):
                nc.scalar.activation(z[:, r : PACK * JH : PACK], pages[r][:].indirect(take_list[:, cols]), COPY)
            nc.vector.quantize_mx(out=z_codes[:].bitcast(FP8X4), scales=z_plane[:], in_=z[:])
            for t in range(N_TILES):
                acc = psum.tile([P, JH], F32, name=f"acc{h}{t}")
                nc.tensor.matmul_mx(
                    out=acc[:],
                    lhsT=w_codes[:, 2 * P * t : 2 * P * (t + 1)].bitcast(FP4X4),
                    lhsT_scale=w_plane[:, P * t : P * (t + 1)],
                    rhs=z_codes[:].bitcast(FP8X4),
                    rhs_scale=z_plane[:],
                    start=True,
                    stop=True,
                )
                sums[h, t] = keep.tile([P, JH], F32, name=f"sums{h}{t}", align_bytes=64)
                nc.vector.tensor_copy(sums[h, t][:], acc[:])

        for h in range(HALVES):
            cols = slice(h * JH // GROUP, (h + 1) * JH // GROUP)
            for t in range(N_TILES):
                nc.scalar.activation(
                    results[t][:].indirect(out_list[:, cols]), sums[h, t][:], COPY, scale=gains[:, t : t + 1]
                )
        for t in range(N_TILES):
            nc.sync.dma_start(out[P * t : P * (t + 1), :], results[t][:])
